import numpy as np
import ml_dtypes


def mxq(x, axis, fmt="e4m3"):
    dtype, down = {"e4m3": (ml_dtypes.float8_e4m3fn, 7), "e5m2": (ml_dtypes.float8_e5m2, 14)}[fmt]
    v = np.moveaxis(np.asarray(x, np.float32).astype(ml_dtypes.bfloat16).astype(np.float64), axis, -1)
    blocks = v.reshape(v.shape[:-1] + (-1, 32))
    amax = np.abs(blocks).max(-1, keepdims=True)
    byte = np.maximum(np.where(amax > 0, np.frexp(amax)[1] - 1 + 127, 0) - down, 1)
    scale = np.exp2(byte - 127.0)
    codes = (blocks / scale).astype(np.float32).astype(dtype).astype(np.float64)
    return np.moveaxis((codes * scale).reshape(v.shape), -1, axis)


WIDE = False


def mx_kscale(k):
    if not WIDE:
        return np.ones(k)
    levels = np.array([10, -10, 5, -5, 0])
    if k % 512:
        return np.exp2(np.random.permutation(np.resize(levels, k // 32))).repeat(32)
    a = np.empty((k // 512, 16))
    for p in range(k // 512):
        a[p, :8] = np.random.permutation(np.resize(levels, 8))
        for g in range(8):
            far = levels[np.abs(levels - a[p, g]) >= 10]
            a[p, g + 8] = far[np.random.randint(len(far))]
    return np.exp2(a.ravel()).repeat(32)


def f64(x):
    return np.asarray(x).astype(np.float64)


def striped(idx):
    return np.tile(idx.reshape(-1, 16).T, (8, 1)).astype(np.uint16)


def unstriped(offs):
    return offs[:16].T.reshape(-1).astype(np.int64)


E2M1 = np.array([0.0, 0.5, 1.0, 1.5, 2.0, 3.0, 4.0, 6.0, -0.0, -0.5, -1.0, -1.5, -2.0, -3.0, -4.0, -6.0])


def pack_weight(w, fmt):
    k, n = w.shape
    w = f64(np.asarray(w, np.float32).astype(ml_dtypes.bfloat16)).reshape(k // 32, 32, n)
    amax = np.abs(w).max(1)
    if fmt == "e4m3":
        byte = np.frexp(amax)[1] - 1 + 127 - 7
    else:
        mant, ex = np.frexp(amax / 6.0)
        byte = np.where(mant > 0.5, ex, ex - 1) + 127
    byte = np.clip(np.where(amax > 0, byte, 1), 1, 254)
    scaled = (w * np.exp2(127.0 - byte)[:, None, :]).reshape(k, n).astype(np.float32)
    by_word = np.ascontiguousarray(scaled.reshape(k // 512, 128, 4, n).transpose(0, 1, 3, 2))
    if fmt == "e4m3":
        words = by_word.astype(ml_dtypes.float8_e4m3fn).view(np.uint8)
    else:
        c = by_word.astype(ml_dtypes.float4_e2m1fn).view(np.uint8) & 0xF
        words = (c[..., 0::2] | (c[..., 1::2] << 4)).reshape(k // 512, 128, 2 * n)
    return np.ascontiguousarray(words), np.ascontiguousarray(byte.astype(np.uint8).reshape(k // 512, 16, n))


def unpack_weight(words, scales, fmt):
    g, _, n = scales.shape
    words = np.ascontiguousarray(words).reshape(g, 128, n, -1)
    if fmt == "e4m3":
        vals = words.view(ml_dtypes.float8_e4m3fn).astype(np.float64)
    else:
        nib = np.empty((g, 128, n, 4), np.uint8)
        nib[..., 0::2] = words & 0xF
        nib[..., 1::2] = words >> 4
        vals = E2M1[nib]
    vals = vals * np.repeat(np.exp2(scales.astype(np.float64) - 127.0), 8, axis=1)[..., None]
    return vals.transpose(0, 1, 3, 2).reshape(g * 512, n)


def pack_table(v):
    words, scales = pack_weight(v, "e4m3")
    return np.concatenate([words.reshape(words.shape[0], -1), scales.reshape(scales.shape[0], -1)], axis=1)


def unpack_table(tab):
    g, t = tab.shape[0], tab.shape[1] // 528
    return unpack_weight(tab[:, :512 * t].reshape(g, 128, t, 4), tab[:, 512 * t:].reshape(g, 16, t), "e4m3")


K, H, M, T, S = 512, 1536, 512, 2048, 1024


def setup_inputs():
    n = np.random.standard_normal
    s = mx_kscale(K)[:, None]
    u = mx_kscale(H)[:, None]
    w2 = 1.4 * n((H, M)) / np.sqrt(H) / u
    p_w8 = pack_weight(w2[:512], "e4m3")
    p_w4 = pack_weight(w2[512:], "e2m1")
    return {
        "tab": pack_table(n((K, T)) * s),
        "w1": (n((K, H)) / np.sqrt(K) / s * u.T).astype(np.float32),
        "w8_words": p_w8[0],
        "w8_scales": p_w8[1],
        "w4_words": p_w4[0],
        "w4_scales": p_w4[1],
        "offs": striped(np.random.permutation(T)[:S]),
    }


def reference(tab, w1, w8_words, w8_scales, w4_words, w4_scales, offs):
    tab_ = unpack_table(tab)[:, unstriped(offs)]
    w1_ = mxq(f64(w1), 0, "e4m3")
    w8_ = unpack_weight(w8_words, w8_scales, "e4m3")
    w4_ = unpack_weight(w4_words, w4_scales, "e2m1")
    h_ = mxq(np.maximum(w1_.T @ tab_, 0.0), 0, "e4m3")
    y = w8_.T @ h_[:512] + w4_.T @ h_[512:]
    return y

@@ -1,0 +1,219 @@
+from contextlib import ExitStack
+
+import concourse.mybir as mybir
+
+K, H, M, T, S = 512, 1536, 512, 2048, 1024
+FLOPS = 2 * S * (K * H + H * M)
+
+F32 = mybir.dt.float32
+BF16 = mybir.dt.bfloat16
+I32 = mybir.dt.int32
+U32 = mybir.dt.uint32
+U16 = mybir.dt.uint16
+U8 = mybir.dt.uint8
+E4M3 = mybir.dt.float8_e4m3fn_x4
+E2M1 = mybir.dt.float4_e2m1fn_x4
+RELU = mybir.ActivationFunctionType.Relu
+
+P = 128
+PACK = 4
+BLOCK = P * PACK
+N_BLOCKS = H // BLOCK
+HALF = 512
+CHUNK = 128
+CHUNKS = HALF // CHUNK
+M_TILES = M // P
+
+LAY = {0: "SSSV", 1: "VV", 2: "VV"}
+RELU_ON = {(0, 0): "SSSS", (1, 0): "SSSV", (0, 1): "SSSV", (1, 1): "SSSS", (0, 2): "SVSS", (1, 2): "SVSV"}
+W1_PIECES = (2, 1, 1)
+OUT_ON = {0: "SVSS", 1: "SVSV"}
+
+
+def tile_list_tabmlp_mix_none_kernel(tc, tab, w1, w8_words, w8_scales, w4_words, w4_scales, offs, out):
+    nc = tc.nc
+    with ExitStack() as ctx:
+        keep = ctx.enter_context(tc.tile_pool(name="keep", bufs=1))
+        psum_h = ctx.enter_context(tc.psum_pool(name="psum_h", bufs=4))
+        psum_o = ctx.enter_context(tc.psum_pool(name="psum_o", bufs=4))
+        store = ctx.enter_context(tc.tile_pool(name="store", bufs=8))
+
+        offsets = keep.tile([P, S // 16], U16, name="offsets")
+        nc.sync.dma_start(offsets[:], offs)
+
+        tab_scales = keep.tile([P, T // 4], I32, name="tab_scales", align_bytes=64)
+        nc.gpsimd.memset(tab_scales[:], 0)
+        warm = keep.tile([P, 1], F32, name="warm")
+        warm_out = keep.tile([P, 1], F32, name="warm_out")
+        nc.vector.memset(warm[:], 0.0)
+        nc.scalar.activation(out=warm_out[:], in_=warm[:], func=RELU)
+
+        tab_words = keep.tile([P, T], I32, name="tab_words", align_bytes=64)
+        w_raw = [keep.tile([P, PACK, BLOCK], F32, name=f"w_raw{b}") for b in range(N_BLOCKS)]
+        w8 = keep.tile([P, M], U32, name="w8", align_bytes=64)
+        w4 = keep.tile([P, 2, 2 * M], U8, name="w4", align_bytes=64)
+        nc.gpsimd.memset(tab_words[:, 0:8], 0)
+        nc.gpsimd.memset(w_raw[0][:, 0, 0:512:256], 0.0)
+        nc.gpsimd.memset(w_raw[1][:, 0, 0:8], 0.0)
+        nc.gpsimd.memset(w8[:, 0:8].bitcast(I32), 0)
+        nc.gpsimd.memset(w_raw[2][:, 0, 0:8], 0.0)
+        nc.gpsimd.memset(w4[:, 0, 0:32].bitcast(I32), 0)
+
+        w_scales = keep.tile([P, N_BLOCKS, M], U8, name="w_scales", align_bytes=64)
+        nc.gpsimd.memset(w_scales[:].rearrange("p a n -> p (a n)").bitcast(I32), 0)
+
+        scale_rows = tab[0:1, 512 * T : 528 * T].rearrange("o (q t) -> (o q) t", q=16).bitcast(I32)
+        for q in range(4):
+            nc.sync.dma_start(tab_scales[32 * q : 32 * q + 4, :], scale_rows[4 * q : 4 * q + 4, :])
+        nc.sync.dma_start(tab_words[:], tab[0:1, 0 : 512 * T].rearrange("o (p x) -> (o p) x", p=P).bitcast(I32))
+
+        w1_rows = w1.rearrange("(p j) r -> p j r", j=PACK)
+
+        def load_w1(b, pieces):
+            width = BLOCK // pieces
+            for i in range(pieces):
+                nc.sync.dma_start(
+                    w_raw[b][:, :, i * width : (i + 1) * width],
+                    w1_rows[:, :, b * BLOCK + i * width : b * BLOCK + (i + 1) * width],
+                )
+
+        load_w1(0, W1_PIECES[0])
+        load_w1(1, W1_PIECES[1])
+        for q in range(4):
+            rows = slice(4 * q, 4 * q + 4)
+            nc.sync.dma_start(
+                w_scales[32 * q : 32 * q + 4, 0, :].bitcast(I32),
+                w8_scales[0, rows, :].bitcast(I32),
+            )
+            nc.gpsimd.dma_start(
+                w_scales[32 * q : 32 * q + 4, 1:3, :].bitcast(I32),
+                w4_scales[:, rows, :].rearrange("a q n -> q a n").bitcast(I32),
+            )
+        nc.sync.dma_start(w8[:].bitcast(I32), w8_words.rearrange("a p n i -> (a p) (n i)").bitcast(I32))
+        load_w1(2, W1_PIECES[2])
+        nc.sync.dma_start(w4[:].bitcast(I32), w4_words.rearrange("a p x -> p a x").bitcast(I32))
+
+        x_codes = [keep.tile([P, HALF], U32, name=f"x_codes{i}", align_bytes=64) for i in range(2)]
+        x_scales = [keep.tile([P, HALF], U8, name=f"x_scales{i}", align_bytes=64) for i in range(2)]
+
+        def look_up(half, dst, window, pieces):
+            n = HALF // pieces
+            for i in range(pieces):
+                first = (half * HALF + i * n) // 16
+                part = offsets[:, first : first + n // 16]
+                nc.vector.tensor_copy(dst[half][:, i * n : (i + 1) * n], window.indirect(part))
+
+
+        w_lay = [keep.tile([P, PACK * BLOCK], BF16, name=f"w_lay{b}", align_bytes=64) for b in range(N_BLOCKS)]
+        w1_codes = [keep.tile([P, BLOCK], U32, name=f"w1_codes{b}", align_bytes=64) for b in range(N_BLOCKS)]
+        w1_scales = [keep.tile([P, BLOCK], U8, name=f"w1_scales{b}", align_bytes=64) for b in range(N_BLOCKS)]
+
+        def lay_out_w1(b):
+            dst = w_lay[b][:].rearrange("p (t m j) -> p m j t", t=PACK, j=PACK)
+            src = w_raw[b][:].rearrange("p j (m t) -> p m j t", t=PACK)
+            n = P // len(LAY[b])
+            for i, engine in enumerate(LAY[b]):
+                ms = slice(i * n, (i + 1) * n)
+                if engine == "S":
+                    nc.scalar.copy(out=dst[:, ms], in_=src[:, ms])
+                else:
+                    nc.vector.tensor_copy(out=dst[:, ms], in_=src[:, ms])
+
+        def quantize_w1(b):
+            for i in range(2):
+                cols = slice(i * BLOCK // 2, (i + 1) * BLOCK // 2)
+                nc.vector.quantize_mx(
+                    out=w1_codes[b][:, cols].bitcast(E4M3),
+                    scales=w1_scales[b][:, cols],
+                    in_=w_lay[b][:, i * 2 * BLOCK : (i + 1) * 2 * BLOCK],
+                )
+
+        h_lay = {}
+        h_codes = {}
+        h_scales = {}
+
+        def hidden(half, b):
+            lay = keep.tile([P, HALF, PACK], BF16, name=f"h_lay{half}{b}", align_bytes=64)
+            codes = keep.tile([P, HALF], U32, name=f"h_codes{half}{b}", align_bytes=64)
+            scales = keep.tile([P, HALF], U8, name=f"h_scales{half}{b}", align_bytes=64)
+            h_codes[half, b], h_scales[half, b] = codes, scales
+            for c in range(CHUNKS):
+                tokens = slice(c * CHUNK, (c + 1) * CHUNK)
+                bank = psum_h.tile([P, PACK, CHUNK], F32, name="bank_h")
+                for t in range(PACK):
+                    cols = slice(t * P, (t + 1) * P)
+                    nc.tensor.matmul_mx(
+                        out=bank[:, t, :],
+                        lhsT=w1_codes[b][:, cols].bitcast(E4M3),
+                        lhsT_scale=w1_scales[b][:, cols],
+                        rhs=x_codes[half][:, tokens].bitcast(E4M3),
+                        rhs_scale=x_scales[half][:, tokens],
+                        start=True,
+                        stop=True,
+                    )
+                by_token = bank[:].rearrange("p t n -> p n t")
+                if RELU_ON[half, b][c] == "S":
+                    nc.scalar.activation(out=lay[:, tokens, :], in_=by_token, func=RELU)
+                else:
+                    nc.vector.tensor_scalar_max(lay[:, tokens, :], by_token, 0.0)
+                if c % 2 == 1:
+                    pair = slice((c - 1) * CHUNK, (c + 1) * CHUNK)
+                    nc.vector.quantize_mx(
+                        out=codes[:, pair].bitcast(E4M3),
+                        scales=scales[:, pair],
+                        in_=lay[:, pair, :].rearrange("p n t -> p (n t)"),
+                    )
+
+        banks_o = {}
+
+        def project(half, b):
+            for n in range(M_TILES):
+                if b == 0:
+                    banks_o[half, n] = psum_o.tile([P, HALF], F32, name="bank_o")
+                if b == 0:
+                    lhsT = w8[:, n * P : (n + 1) * P].bitcast(E4M3)
+                else:
+                    lhsT = w4[:, b - 1, 2 * n * P : 2 * (n + 1) * P].bitcast(E2M1)
+                nc.tensor.matmul_mx(
+                    out=banks_o[half, n][:],
+                    lhsT=lhsT,
+                    lhsT_scale=w_scales[:, b, n * P : (n + 1) * P],
+                    rhs=h_codes[half, b][:].bitcast(E4M3),
+                    rhs_scale=h_scales[half, b][:],
+                    start=(b == 0),
+                    stop=(b == N_BLOCKS - 1),
+                )
+
+        def emit(half):
+            for n in range(M_TILES):
+                result = store.tile([P, HALF], F32, name="result")
+                if OUT_ON[half][n] == "S":
+                    nc.scalar.copy(out=result[:], in_=banks_o[half, n][:])
+                else:
+                    nc.vector.tensor_copy(out=result[:], in_=banks_o[half, n][:])
+                nc.sync.dma_start(out[n * P : (n + 1) * P, half * HALF : (half + 1) * HALF], result[:])
+
+        look_up(0, x_scales, tab_scales[:].bitcast(U8), 1)
+        look_up(1, x_scales, tab_scales[:].bitcast(U8), 1)
+        look_up(0, x_codes, tab_words[:].bitcast(U32), 1)
+        lay_out_w1(0)
+        quantize_w1(0)
+        look_up(1, x_codes, tab_words[:].bitcast(U32), 2)
+        hidden(0, 0)
+        hidden(1, 0)
+        lay_out_w1(1)
+        quantize_w1(1)
+        hidden(0, 1)
+        project(0, 0)
+        hidden(1, 1)
+        lay_out_w1(2)
+        quantize_w1(2)
+        hidden(0, 2)
+        project(0, 1)
+        hidden(1, 2)
+        project(0, 2)
+        emit(0)
+        project(1, 0)
+        project(1, 1)
+        project(1, 2)
+        emit(1)

@@ -24,9 +24,10 @@ CHUNK = 128
 CHUNKS = HALF // CHUNK
 M_TILES = M // P
 
-LAY = {0: "SSSV", 1: "VV", 2: "VV"}
-RELU_ON = {(0, 0): "SSSS", (1, 0): "SSSV", (0, 1): "SSSV", (1, 1): "SSSS", (0, 2): "SVSS", (1, 2): "SVSV"}
-W1_PIECES = (2, 1, 1)
+WARM_UP = 3
+PIECES = (2, 1, 1)
+LAY = {(0, 0): "SS", (0, 1): "SS", (1, 0): "VV", (2, 0): "VV"}
+RELU_ON = {(0, 0): "SSSS", (1, 0): "SSVS", (0, 1): "SSSS", (1, 1): "SSVV", (0, 2): "SVSS", (1, 2): "SVSV"}
 OUT_ON = {0: "SVSS", 1: "SVSV"}
 
 
@@ -34,63 +35,66 @@ def tile_list_tabmlp_mix_none_kernel(tc, tab, w1, w8_words, w8_scales, w4_words,
     nc = tc.nc
     with ExitStack() as ctx:
         keep = ctx.enter_context(tc.tile_pool(name="keep", bufs=1))
-        psum_h = ctx.enter_context(tc.psum_pool(name="psum_h", bufs=4))
-        psum_o = ctx.enter_context(tc.psum_pool(name="psum_o", bufs=4))
+        psum_h = ctx.enter_context(tc.psum_pool(name="psum_h", bufs=5))
+        psum_o = ctx.enter_context(tc.psum_pool(name="psum_o", bufs=3))
         store = ctx.enter_context(tc.tile_pool(name="store", bufs=8))
 
         offsets = keep.tile([P, S // 16], U16, name="offsets")
         nc.sync.dma_start(offsets[:], offs)
 
         tab_scales = keep.tile([P, T // 4], I32, name="tab_scales", align_bytes=64)
-        nc.gpsimd.memset(tab_scales[:], 0)
+        nc.gpsimd.memset(tab_scales[:, 0 : T // 8], 0)
+        nc.vector.memset(tab_scales[:, T // 8 : T // 4], 0)
         warm = keep.tile([P, 1], F32, name="warm")
         warm_out = keep.tile([P, 1], F32, name="warm_out")
         nc.vector.memset(warm[:], 0.0)
         nc.scalar.activation(out=warm_out[:], in_=warm[:], func=RELU)
 
         tab_words = keep.tile([P, T], I32, name="tab_words", align_bytes=64)
-        w_raw = [keep.tile([P, PACK, BLOCK], F32, name=f"w_raw{b}") for b in range(N_BLOCKS)]
+        w_raw = {}
+        for b, pieces in enumerate(PIECES):
+            for i in range(pieces):
+                w_raw[b, i] = keep.tile([P, PACK, BLOCK // pieces], F32, name=f"w_raw{b}{i}")
         w8 = keep.tile([P, M], U32, name="w8", align_bytes=64)
         w4 = keep.tile([P, 2, 2 * M], U8, name="w4", align_bytes=64)
         nc.gpsimd.memset(tab_words[:, 0:8], 0)
-        nc.gpsimd.memset(w_raw[0][:, 0, 0:512:256], 0.0)
-        nc.gpsimd.memset(w_raw[1][:, 0, 0:8], 0.0)
+        nc.gpsimd.memset(w_raw[0, 1][:, 0, 0:8], 0.0)
+        nc.gpsimd.memset(w_raw[1, 0][:, 0, 0:8], 0.0)
+        nc.gpsimd.memset(w_raw[2, 0][:, 0, 0:8], 0.0)
         nc.gpsimd.memset(w8[:, 0:8].bitcast(I32), 0)
-        nc.gpsimd.memset(w_raw[2][:, 0, 0:8], 0.0)
         nc.gpsimd.memset(w4[:, 0, 0:32].bitcast(I32), 0)
 
         w_scales = keep.tile([P, N_BLOCKS, M], U8, name="w_scales", align_bytes=64)
         nc.gpsimd.memset(w_scales[:].rearrange("p a n -> p (a n)").bitcast(I32), 0)
 
+        w1_rows = w1.rearrange("(p j) r -> p j r", j=PACK)
+
+        def load_w1(b, i):
+            width = BLOCK // PIECES[b]
+            first = b * BLOCK + i * width
+            nc.sync.dma_start(w_raw[b, i][:], w1_rows[:, :, first : first + width])
+
+        load_w1(0, 0)
         scale_rows = tab[0:1, 512 * T : 528 * T].rearrange("o (q t) -> (o q) t", q=16).bitcast(I32)
         for q in range(4):
             nc.sync.dma_start(tab_scales[32 * q : 32 * q + 4, :], scale_rows[4 * q : 4 * q + 4, :])
         nc.sync.dma_start(tab_words[:], tab[0:1, 0 : 512 * T].rearrange("o (p x) -> (o p) x", p=P).bitcast(I32))
-
-        w1_rows = w1.rearrange("(p j) r -> p j r", j=PACK)
-
-        def load_w1(b, pieces):
-            width = BLOCK // pieces
-            for i in range(pieces):
-                nc.sync.dma_start(
-                    w_raw[b][:, :, i * width : (i + 1) * width],
-                    w1_rows[:, :, b * BLOCK + i * width : b * BLOCK + (i + 1) * width],
-                )
-
-        load_w1(0, W1_PIECES[0])
-        load_w1(1, W1_PIECES[1])
+        load_w1(0, 1)
+        load_w1(1, 0)
+        load_w1(2, 0)
         for q in range(4):
             rows = slice(4 * q, 4 * q + 4)
             nc.sync.dma_start(
                 w_scales[32 * q : 32 * q + 4, 0, :].bitcast(I32),
                 w8_scales[0, rows, :].bitcast(I32),
             )
-            nc.gpsimd.dma_start(
+        nc.sync.dma_start(w8[:].bitcast(I32), w8_words.rearrange("a p n i -> (a p) (n i)").bitcast(I32))
+        for q in range(4):
+            rows = slice(4 * q, 4 * q + 4)
+            nc.sync.dma_start(
                 w_scales[32 * q : 32 * q + 4, 1:3, :].bitcast(I32),
                 w4_scales[:, rows, :].rearrange("a q n -> q a n").bitcast(I32),
             )
-        nc.sync.dma_start(w8[:].bitcast(I32), w8_words.rearrange("a p n i -> (a p) (n i)").bitcast(I32))
-        load_w1(2, W1_PIECES[2])
         nc.sync.dma_start(w4[:].bitcast(I32), w4_words.rearrange("a p x -> p a x").bitcast(I32))
 
         x_codes = [keep.tile([P, HALF], U32, name=f"x_codes{i}", align_bytes=64) for i in range(2)]
@@ -104,20 +108,35 @@ def tile_list_tabmlp_mix_none_kernel(tc, tab, w1, w8_words, w8_scales, w4_words,
                 nc.vector.tensor_copy(dst[half][:, i * n : (i + 1) * n], window.indirect(part))
 
 
+        def warm_up():
+            bank = psum_o.tile([P, HALF], F32, name="bank_o")
+            for i in range(WARM_UP):
+                nc.tensor.matmul_mx(
+                    out=bank[:],
+                    lhsT=x_codes[0][:, 0:P].bitcast(E4M3),
+                    lhsT_scale=x_scales[0][:, 0:P],
+                    rhs=x_codes[0][:].bitcast(E4M3),
+                    rhs_scale=x_scales[0][:],
+                    start=True,
+                    stop=True,
+                )
+
         w_lay = [keep.tile([P, PACK * BLOCK], BF16, name=f"w_lay{b}", align_bytes=64) for b in range(N_BLOCKS)]
         w1_codes = [keep.tile([P, BLOCK], U32, name=f"w1_codes{b}", align_bytes=64) for b in range(N_BLOCKS)]
         w1_scales = [keep.tile([P, BLOCK], U8, name=f"w1_scales{b}", align_bytes=64) for b in range(N_BLOCKS)]
 
         def lay_out_w1(b):
             dst = w_lay[b][:].rearrange("p (t m j) -> p m j t", t=PACK, j=PACK)
-            src = w_raw[b][:].rearrange("p j (m t) -> p m j t", t=PACK)
-            n = P // len(LAY[b])
-            for i, engine in enumerate(LAY[b]):
-                ms = slice(i * n, (i + 1) * n)
-                if engine == "S":
-                    nc.scalar.copy(out=dst[:, ms], in_=src[:, ms])
-                else:
-                    nc.vector.tensor_copy(out=dst[:, ms], in_=src[:, ms])
+            for piece in range(PIECES[b]):
+                src = w_raw[b, piece][:].rearrange("p j (m t) -> p m j t", t=PACK)
+                engines = LAY[b, piece]
+                n = P // PIECES[b] // len(engines)
+                for i, engine in enumerate(engines):
+                    to = slice((piece * len(engines) + i) * n, (piece * len(engines) + i + 1) * n)
+                    if engine == "S":
+                        nc.scalar.copy(out=dst[:, to], in_=src[:, i * n : (i + 1) * n])
+                    else:
+                        nc.vector.tensor_copy(out=dst[:, to], in_=src[:, i * n : (i + 1) * n])
 
         def quantize_w1(b):
             for i in range(2):
@@ -196,23 +215,24 @@ def tile_list_tabmlp_mix_none_kernel(tc, tab, w1, w8_words, w8_scales, w4_words,
         look_up(0, x_scales, tab_scales[:].bitcast(U8), 1)
         look_up(1, x_scales, tab_scales[:].bitcast(U8), 1)
         look_up(0, x_codes, tab_words[:].bitcast(U32), 1)
+        warm_up()
+        look_up(1, x_codes, tab_words[:].bitcast(U32), 1)
         lay_out_w1(0)
         quantize_w1(0)
-        look_up(1, x_codes, tab_words[:].bitcast(U32), 2)
-        hidden(0, 0)
-        hidden(1, 0)
         lay_out_w1(1)
         quantize_w1(1)
-        hidden(0, 1)
-        project(0, 0)
-        hidden(1, 1)
         lay_out_w1(2)
         quantize_w1(2)
+        hidden(0, 0)
+        hidden(1, 0)
+        hidden(0, 1)
+        project(0, 0)
         hidden(0, 2)
         project(0, 1)
-        hidden(1, 2)
         project(0, 2)
+        hidden(1, 1)
         emit(0)
+        hidden(1, 2)
         project(1, 0)
         project(1, 1)
         project(1, 2)

@@ -27,7 +27,7 @@ M_TILES = M // P
 WARM_UP = 3
 PIECES = (2, 1, 1)
 LAY = {(0, 0): "SS", (0, 1): "SS", (1, 0): "VV", (2, 0): "VV"}
-RELU_ON = {(0, 0): "SSSS", (1, 0): "SSVS", (0, 1): "SSSS", (1, 1): "SSVV", (0, 2): "SVSS", (1, 2): "SVSV"}
+RELU_ON = {(0, 0): "SSSS", (1, 0): "SSVS", (0, 1): "SSSS", (1, 1): "SSVS", (0, 2): "VSSS", (1, 2): "VSVS"}
 OUT_ON = {0: "SVSS", 1: "SVSV"}
 
 
@@ -206,6 +206,12 @@ def tile_list_tabmlp_mix_none_kernel(tc, tab, w1, w8_words, w8_scales, w4_words,
         def emit(half):
             for n in range(M_TILES):
                 result = store.tile([P, HALF], F32, name="result")
+                if half == 1 and n == M_TILES - 1:
+                    mid = HALF // 2
+                    for cols in (slice(0, mid), slice(mid, HALF)):
+                        nc.vector.tensor_copy(out=result[:, cols], in_=banks_o[half, n][:, cols])
+                        nc.sync.dma_start(out[n * P : (n + 1) * P, HALF + cols.start : HALF + cols.stop], result[:, cols])
+                    continue
                 if OUT_ON[half][n] == "S":
                     nc.scalar.copy(out=result[:], in_=banks_o[half, n][:])
                 else:

from contextlib import ExitStack

import concourse.mybir as mybir

K, H, M, T, S = 512, 1536, 512, 2048, 1024
FLOPS = 2 * S * (K * H + H * M)

F32 = mybir.dt.float32
BF16 = mybir.dt.bfloat16
I32 = mybir.dt.int32
U32 = mybir.dt.uint32
U16 = mybir.dt.uint16
U8 = mybir.dt.uint8
E4M3 = mybir.dt.float8_e4m3fn_x4
E2M1 = mybir.dt.float4_e2m1fn_x4
RELU = mybir.ActivationFunctionType.Relu

P = 128
PACK = 4
BLOCK = P * PACK
N_BLOCKS = H // BLOCK
HALF = 512
CHUNK = 128
CHUNKS = HALF // CHUNK
M_TILES = M // P

WARM_UP = 3
PIECES = (2, 1, 1)
LAY = {(0, 0): "SS", (0, 1): "SS", (1, 0): "VV", (2, 0): "VV"}
RELU_ON = {(0, 0): "SSSS", (1, 0): "SSVS", (0, 1): "SSSS", (1, 1): "SSVS", (0, 2): "VSSS", (1, 2): "VSVS"}
OUT_ON = {0: "SVSS", 1: "SVSV"}


def tile_list_tabmlp_mix_none_kernel(tc, tab, w1, w8_words, w8_scales, w4_words, w4_scales, offs, out):
    nc = tc.nc
    with ExitStack() as ctx:
        keep = ctx.enter_context(tc.tile_pool(name="keep", bufs=1))
        psum_h = ctx.enter_context(tc.psum_pool(name="psum_h", bufs=5))
        psum_o = ctx.enter_context(tc.psum_pool(name="psum_o", bufs=3))
        store = ctx.enter_context(tc.tile_pool(name="store", bufs=8))

        offsets = keep.tile([P, S // 16], U16, name="offsets")
        nc.sync.dma_start(offsets[:], offs)

        tab_scales = keep.tile([P, T // 4], I32, name="tab_scales", align_bytes=64)
        nc.gpsimd.memset(tab_scales[:, 0 : T // 8], 0)
        nc.vector.memset(tab_scales[:, T // 8 : T // 4], 0)
        warm = keep.tile([P, 1], F32, name="warm")
        warm_out = keep.tile([P, 1], F32, name="warm_out")
        nc.vector.memset(warm[:], 0.0)
        nc.scalar.activation(out=warm_out[:], in_=warm[:], func=RELU)

        tab_words = keep.tile([P, T], I32, name="tab_words", align_bytes=64)
        w_raw = {}
        for b, pieces in enumerate(PIECES):
            for i in range(pieces):
                w_raw[b, i] = keep.tile([P, PACK, BLOCK // pieces], F32, name=f"w_raw{b}{i}")
        w8 = keep.tile([P, M], U32, name="w8", align_bytes=64)
        w4 = keep.tile([P, 2, 2 * M], U8, name="w4", align_bytes=64)
        nc.gpsimd.memset(tab_words[:, 0:8], 0)
        nc.gpsimd.memset(w_raw[0, 1][:, 0, 0:8], 0.0)
        nc.gpsimd.memset(w_raw[1, 0][:, 0, 0:8], 0.0)
        nc.gpsimd.memset(w_raw[2, 0][:, 0, 0:8], 0.0)
        nc.gpsimd.memset(w8[:, 0:8].bitcast(I32), 0)
        nc.gpsimd.memset(w4[:, 0, 0:32].bitcast(I32), 0)

        w_scales = keep.tile([P, N_BLOCKS, M], U8, name="w_scales", align_bytes=64)
        nc.gpsimd.memset(w_scales[:].rearrange("p a n -> p (a n)").bitcast(I32), 0)

        w1_rows = w1.rearrange("(p j) r -> p j r", j=PACK)

        def load_w1(b, i):
            width = BLOCK // PIECES[b]
            first = b * BLOCK + i * width
            nc.sync.dma_start(w_raw[b, i][:], w1_rows[:, :, first : first + width])

        load_w1(0, 0)
        scale_rows = tab[0:1, 512 * T : 528 * T].rearrange("o (q t) -> (o q) t", q=16).bitcast(I32)
        for q in range(4):
            nc.sync.dma_start(tab_scales[32 * q : 32 * q + 4, :], scale_rows[4 * q : 4 * q + 4, :])
        nc.sync.dma_start(tab_words[:], tab[0:1, 0 : 512 * T].rearrange("o (p x) -> (o p) x", p=P).bitcast(I32))
        load_w1(0, 1)
        load_w1(1, 0)
        load_w1(2, 0)
        for q in range(4):
            rows = slice(4 * q, 4 * q + 4)
            nc.sync.dma_start(
                w_scales[32 * q : 32 * q + 4, 0, :].bitcast(I32),
                w8_scales[0, rows, :].bitcast(I32),
            )
        nc.sync.dma_start(w8[:].bitcast(I32), w8_words.rearrange("a p n i -> (a p) (n i)").bitcast(I32))
        for q in range(4):
            rows = slice(4 * q, 4 * q + 4)
            nc.sync.dma_start(
                w_scales[32 * q : 32 * q + 4, 1:3, :].bitcast(I32),
                w4_scales[:, rows, :].rearrange("a q n -> q a n").bitcast(I32),
            )
        nc.sync.dma_start(w4[:].bitcast(I32), w4_words.rearrange("a p x -> p a x").bitcast(I32))

        x_codes = [keep.tile([P, HALF], U32, name=f"x_codes{i}", align_bytes=64) for i in range(2)]
        x_scales = [keep.tile([P, HALF], U8, name=f"x_scales{i}", align_bytes=64) for i in range(2)]

        def look_up(half, dst, window, pieces):
            n = HALF // pieces
            for i in range(pieces):
                first = (half * HALF + i * n) // 16
                part = offsets[:, first : first + n // 16]
                nc.vector.tensor_copy(dst[half][:, i * n : (i + 1) * n], window.indirect(part))


        def warm_up():
            bank = psum_o.tile([P, HALF], F32, name="bank_o")
            for i in range(WARM_UP):
                nc.tensor.matmul_mx(
                    out=bank[:],
                    lhsT=x_codes[0][:, 0:P].bitcast(E4M3),
                    lhsT_scale=x_scales[0][:, 0:P],
                    rhs=x_codes[0][:].bitcast(E4M3),
                    rhs_scale=x_scales[0][:],
                    start=True,
                    stop=True,
                )

        w_lay = [keep.tile([P, PACK * BLOCK], BF16, name=f"w_lay{b}", align_bytes=64) for b in range(N_BLOCKS)]
        w1_codes = [keep.tile([P, BLOCK], U32, name=f"w1_codes{b}", align_bytes=64) for b in range(N_BLOCKS)]
        w1_scales = [keep.tile([P, BLOCK], U8, name=f"w1_scales{b}", align_bytes=64) for b in range(N_BLOCKS)]

        def lay_out_w1(b):
            dst = w_lay[b][:].rearrange("p (t m j) -> p m j t", t=PACK, j=PACK)
            for piece in range(PIECES[b]):
                src = w_raw[b, piece][:].rearrange("p j (m t) -> p m j t", t=PACK)
                engines = LAY[b, piece]
                n = P // PIECES[b] // len(engines)
                for i, engine in enumerate(engines):
                    to = slice((piece * len(engines) + i) * n, (piece * len(engines) + i + 1) * n)
                    if engine == "S":
                        nc.scalar.copy(out=dst[:, to], in_=src[:, i * n : (i + 1) * n])
                    else:
                        nc.vector.tensor_copy(out=dst[:, to], in_=src[:, i * n : (i + 1) * n])

        def quantize_w1(b):
            for i in range(2):
                cols = slice(i * BLOCK // 2, (i + 1) * BLOCK // 2)
                nc.vector.quantize_mx(
                    out=w1_codes[b][:, cols].bitcast(E4M3),
                    scales=w1_scales[b][:, cols],
                    in_=w_lay[b][:, i * 2 * BLOCK : (i + 1) * 2 * BLOCK],
                )

        h_lay = {}
        h_codes = {}
        h_scales = {}

        def hidden(half, b):
            lay = keep.tile([P, HALF, PACK], BF16, name=f"h_lay{half}{b}", align_bytes=64)
            codes = keep.tile([P, HALF], U32, name=f"h_codes{half}{b}", align_bytes=64)
            scales = keep.tile([P, HALF], U8, name=f"h_scales{half}{b}", align_bytes=64)
            h_codes[half, b], h_scales[half, b] = codes, scales
            for c in range(CHUNKS):
                tokens = slice(c * CHUNK, (c + 1) * CHUNK)
                bank = psum_h.tile([P, PACK, CHUNK], F32, name="bank_h")
                for t in range(PACK):
                    cols = slice(t * P, (t + 1) * P)
                    nc.tensor.matmul_mx(
                        out=bank[:, t, :],
                        lhsT=w1_codes[b][:, cols].bitcast(E4M3),
                        lhsT_scale=w1_scales[b][:, cols],
                        rhs=x_codes[half][:, tokens].bitcast(E4M3),
                        rhs_scale=x_scales[half][:, tokens],
                        start=True,
                        stop=True,
                    )
                by_token = bank[:].rearrange("p t n -> p n t")
                if RELU_ON[half, b][c] == "S":
                    nc.scalar.activation(out=lay[:, tokens, :], in_=by_token, func=RELU)
                else:
                    nc.vector.tensor_scalar_max(lay[:, tokens, :], by_token, 0.0)
                if c % 2 == 1:
                    pair = slice((c - 1) * CHUNK, (c + 1) * CHUNK)
                    nc.vector.quantize_mx(
                        out=codes[:, pair].bitcast(E4M3),
                        scales=scales[:, pair],
                        in_=lay[:, pair, :].rearrange("p n t -> p (n t)"),
                    )

        banks_o = {}

        def project(half, b):
            for n in range(M_TILES):
                if b == 0:
                    banks_o[half, n] = psum_o.tile([P, HALF], F32, name="bank_o")
                if b == 0:
                    lhsT = w8[:, n * P : (n + 1) * P].bitcast(E4M3)
                else:
                    lhsT = w4[:, b - 1, 2 * n * P : 2 * (n + 1) * P].bitcast(E2M1)
                nc.tensor.matmul_mx(
                    out=banks_o[half, n][:],
                    lhsT=lhsT,
                    lhsT_scale=w_scales[:, b, n * P : (n + 1) * P],
                    rhs=h_codes[half, b][:].bitcast(E4M3),
                    rhs_scale=h_scales[half, b][:],
                    start=(b == 0),
                    stop=(b == N_BLOCKS - 1),
                )

        def emit(half):
            for n in range(M_TILES):
                result = store.tile([P, HALF], F32, name="result")
                if half == 1 and n == M_TILES - 1:
                    mid = HALF // 2
                    for cols in (slice(0, mid), slice(mid, HALF)):
                        nc.vector.tensor_copy(out=result[:, cols], in_=banks_o[half, n][:, cols])
                        nc.sync.dma_start(out[n * P : (n + 1) * P, HALF + cols.start : HALF + cols.stop], result[:, cols])
                    continue
                if OUT_ON[half][n] == "S":
                    nc.scalar.copy(out=result[:], in_=banks_o[half, n][:])
                else:
                    nc.vector.tensor_copy(out=result[:], in_=banks_o[half, n][:])
                nc.sync.dma_start(out[n * P : (n + 1) * P, half * HALF : (half + 1) * HALF], result[:])

        look_up(0, x_scales, tab_scales[:].bitcast(U8), 1)
        look_up(1, x_scales, tab_scales[:].bitcast(U8), 1)
        look_up(0, x_codes, tab_words[:].bitcast(U32), 1)
        warm_up()
        look_up(1, x_codes, tab_words[:].bitcast(U32), 1)
        lay_out_w1(0)
        quantize_w1(0)
        lay_out_w1(1)
        quantize_w1(1)
        lay_out_w1(2)
        quantize_w1(2)
        hidden(0, 0)
        hidden(1, 0)
        hidden(0, 1)
        project(0, 0)
        hidden(0, 2)
        project(0, 1)
        project(0, 2)
        hidden(1, 1)
        emit(0)
        hidden(1, 2)
        project(1, 0)
        project(1, 1)
        project(1, 2)
        emit(1)
